import numpy as np, ml_dtypes
CORES = [3,7,11,15,131,135,139,143]
N = 8
import mx_ref
BF = ml_dtypes.bfloat16
def tile(rs):
    return np.stack(rs, axis=2).reshape(128, -1).astype(BF)
def cut(t, i, w=512):
    return t[:, w * i:w * i + w]
def pick(q, e):
    c = np.concatenate([q[0].reshape(128, -1, 4), np.zeros((128, 1, 4), np.uint8)], axis=1); s = np.concatenate([q[1], np.ones((16, 1), np.uint8)], axis=1)
    return (np.ascontiguousarray(c[:, e].reshape(128, -1)), np.ascontiguousarray(s[:, e]))
def join(*qs):
    return (np.concatenate([q[0] for q in qs], axis=1), np.concatenate([q[1] for q in qs], axis=1))
def put(q, e, v):
    c, s = q[0].reshape(128, -1, 4).copy(), q[1].copy(); c[:, e] = v[0].reshape(128, -1, 4); s[:, e] = v[1]
    return (c.reshape(128, -1), s)
def pk(c, s):
    return (np.ascontiguousarray(c), mx_ref.live(s))
def emit(q):
    return q[0], q[1]
def packed(v, rng):
    q = [mx_ref.quantize(np.ascontiguousarray(v[r])) for r in range(N)]
    return np.stack([a for a, b in q]), np.stack([mx_ref.plane(b, rng) for a, b in q])
def values_of_codes():
    e, c = np.zeros((128, 128, 4), np.float32), np.zeros((128, 2, 4), np.uint8)
    e[np.arange(128), np.arange(128), 0] = 1
    c[:127, :, 0] = np.arange(256).reshape(2, 128).T[:127]
    return mx_ref.matmul(mx_ref.quantize(e.reshape(128, 512).astype(BF)), (c.reshape(128, 8), np.full((16, 2), 127, np.uint8))).T.reshape(-1).astype(np.float64)
CODE_VALUE, SCALE_VALUE = values_of_codes(), 2.0 ** (np.arange(256) - 127.0)
def decode(q):
    return (CODE_VALUE[q[0]].reshape(16, 8, -1, 4) * SCALE_VALUE[q[1]][:, None, :, None] + 0.0).reshape(128, -1).astype(np.float32)
def f(rng, *shape):
    return mx_ref.flush((rng.standard_normal(shape, dtype=np.float32) * np.exp2(rng.integers(-2, 3, shape[:-1] + (1,)))).astype(BF))
def wide(rng, *shape, cols=0):
    v = rng.standard_normal(shape, dtype=np.float32) * np.exp2(rng.integers(-12, 13, shape)).astype(np.float32)
    if cols: v *= np.repeat(np.exp2(rng.integers(-cols, cols + 1, shape[:-2] + (1, shape[-1] // 4))) * (rng.random(shape[:-2] + (1, shape[-1] // 4)) > 0.0625), 4, axis=-1).astype(np.float32)
    return mx_ref.flush(v.astype(BF))
C, B, K, R = 448, 6, 64, 2
def key_of(s):
    b = (s.reshape(8, 16, C)[:, :B] < 0).astype(np.int64)
    return np.sum(b << np.arange(B)[:, None], axis=1)
def parts(t):
    return t.reshape(8, 16, -1, 4).transpose(0, 2, 1, 3)
def whole(p):
    return np.ascontiguousarray(p.transpose(0, 2, 1, 3)).reshape(128, -1)
def scan(p, key, start):
    h, o, g = np.array(start, np.float32), np.zeros((8, C, 16, 4), np.float32), np.arange(8)
    for j in range(C):
        n = np.maximum(np.float32(0.5) * h[g, key[:, j]], p[:, j])
        h[g, key[:, j]] = n
        o[:, j] = n
    return o, h
def same(a):
    return np.stack([a] * N)
def weights(rng, w):
    c, p = packed(same(w), rng)
    return {"wc": c, "ws": p}
def planted(rng, x, keys, size=np.ones((8, B)), swap=False, add=False, second=None):
    x[:, :, :8] = 0
    for e, k in ((0, keys),) if second is None else ((0, keys), (2, second)):
        for i in range(B):
            bit = k >> i & 1
            x[:, :, i, :, e] = (1 - bit).astype(np.float32).astype(BF)
            x[:, :, i, :, e + 1] = bit.astype(np.float32).astype(BF)
    u = np.zeros((128, 128, 4), np.float32)
    for g in range(8):
        for i in range(B):
            u[16 * g + i, 16 * g + i, 0] = size[g, i]
            u[16 * g + i, 16 * g + i, 1] = -size[g, i]
    w = np.zeros((128, 4, 128, 4), np.float32)
    i = np.arange(128)
    for b in range(4): w[i, b, i, b] = 32
    n = i[i % 16 < 8]
    turn = (1, 0, 2, 3) if swap else (0, 1, 2, 3) if second is None else (2, 3, 0, 1)
    for b in range(4):
        w[n, b, n, b] = 0
        w[n, b, n, turn[b]] = 32
    if add:
        n = i[(i % 16 >= 8) & (i % 16 < 12)]
        for b in range(4): w[n + 4, b, n, b] = 32
    return {"x": x.reshape(N, 128, 4 * C), "u": same(u.reshape(128, 512).astype(BF)), "v": same(np.array(f(rng, 128, 512))), **weights(rng, w.reshape(128, 2048).astype(BF))}
def numbers_of(rng):
    return np.array(f(rng, N, 128, 4 * C)).reshape(N, 8, 16, C, 4)
def three(rng, k, shape=(8, 4)):
    return rng.integers(4, 8, shape) * 2.0 ** k
def setup_inputs(rng):
    return {"x": np.array(f(rng, N, 128, 4 * C)), "u": same(np.array(f(rng, 128, 512))), "v": same(np.array(f(rng, 128, 512))), **weights(rng, np.array(f(rng, 128, 2048)))}
def setup_inputs_long(rng):
    r, j = np.arange(N)[:, None], np.arange(C)[None, :]
    a = rng.permutation(K)
    n = rng.integers(0, K, (N, C))
    third = 3 * rng.integers(0, K // 3, (N, C)) + (-r) % 3
    each = np.stack([rng.permutation(C) % K for i in range(N)])
    alone = np.where(j == rng.integers(0, 48, (N, 1)), 0, K - 1)
    p = [a[0], a[r + 1], a[N + 1 + r % 2], third, each, K - 1 - j * K // C, alone, np.where((r == 0) | (r == N - 1), n, a[N + 3])]
    keys = np.zeros((N, 8, C), int)
    heads = rng.permutation(8)
    for g, q in zip(heads, p): keys[:, g] = q
    first = keys.copy()
    x = numbers_of(rng)
    s = 65 + rng.integers(0, 2) - r * (80 // N)
    s[0] += 8
    for g, large in ((int(heads[0]), (C - 1 - j - s) % 80 == 0), (int(heads[6]), ((C - 1 - j) % 80 == 0) & (j >= 80))):
        first[:, g] = np.where(large, a[1], a[2])
        x[:, g, 8:, :, 2:] = three(rng, -30, (N, 8, C, 2)).astype(np.float32).astype(BF)
        x[:, g, 8:, :, :2] = np.where(large[:, None, :, None], three(rng, 27, (N, 8, C, 2)), 0.0).astype(np.float32).astype(BF)
        x[:, g, 8, :, 0] = np.where(large, 2.0 ** 30, 0.0).astype(np.float32).astype(BF)
    return planted(rng, x, first, second=keys)
def place_in_key(keys):
    o = np.argsort(keys, axis=-1, kind="stable")
    s = np.take_along_axis(keys, o, axis=-1)
    i = np.broadcast_to(np.arange(C), s.shape)
    head = np.ones(s.shape, bool)
    head[..., 1:] = s[..., 1:] != s[..., :-1]
    n = np.zeros(s.shape, int)
    np.put_along_axis(n, o, i - np.maximum.accumulate(np.where(head, i, 0), axis=-1), axis=-1)
    return n
def setup_inputs_near(rng):
    odd = rng.permutation(8) % 2
    size = np.exp2(np.where(odd, 28.0, -28.0))[:, None] * np.ones((8, B))
    low = rng.integers(0, B, 8)
    size[np.arange(8), low] = 0
    keys = rng.integers(0, K, (N, 8, C)) & ~(1 << low)[None, :, None]
    none = [rng.permutation(C)[:2] for r in range(N)]
    for r in range(N): keys[r][:, none[r]] = 0
    x = numbers_of(rng)
    m = (place_in_key(keys) % 2)[:, :, None, :, None]
    s = np.where(m == 0, 2.0, 1.0)
    up = (rng.integers(0, 2, (N, 8, 4, 1, 2)) + m) % 2
    x[:, :, 8:12, :, :2] = s.astype(np.float32).astype(BF)
    x[:, :, 12:, :, :2] = (s * (8 + up) * 2.0 ** -7).astype(np.float32).astype(BF)
    d = planted(rng, x, keys, size, add=True)
    x = d["x"].astype(np.float32).reshape(N, 8, 16, C, 4)
    for g in np.flatnonzero(odd == 0): x[:, g, :8] *= np.float32(2.0 ** -20)
    x = x.astype(BF).reshape(N, 128, C, 4)
    for r in range(N): x[r][:, none[r]] = 0
    return {**d, "x": x.reshape(N, 128, 4 * C)}
def setup_inputs_gone(rng):
    keys = 2 * rng.integers(0, K // 2, (N, 8, C)) + (np.arange(N)[:, None, None] + rng.integers(0, 2, (1, 8, 1))) % 2
    return planted(rng, numbers_of(rng), keys, swap=True)
def step(rng, v, n):
    return v * 2.0 ** -n + rng.choice([-1.0, 1.0], v.shape) * 2.0 ** (19 - n)
def runs(rng, t):
    v, s = three(rng, 20), [three(rng, -8) for i in range(4)]
    if t == 0: return [v] + s
    if t == 1: return s + [v]
    if t == 2: return [v, -2.0 * v] + s[:3]
    return [v] + [step(rng, v, n) for n in range(1, 5)]
def setup_inputs_order(rng):
    x = numbers_of(rng)
    keys = np.zeros((2, N, 8, C), int)
    def plant(r, g, j, k, v):
        keys[:, r, g, j] = k
        x[r, g, 8:, j] = v.astype(np.float32).astype(BF)
    firsts = rng.permutation(8) % (N - 3)
    for g in range(8):
        o = rng.permutation(K)
        keys[:, :, g] = o[9 + rng.integers(0, K - 9, (N, C))]
        at = [rng.permutation(C) for r in range(N)]
        for t in (0, 2):
            first = int(rng.integers(0, N - 1)) if g % 2 else 0
            v = three(rng, 20)
            plant(first, g, at[first][t], o[t], v)
            for r in range(first + 1, N): plant(r, g, at[r][t], o[t], three(rng, -8) if t == 0 else step(rng, v, r - first))
        a, b = 0, N - 1
        if g % 4:
            a = int(rng.integers(0, N - 2))
            b = int(rng.integers(a + 2, N))
        plant(a, g, at[a][1], o[1], three(rng, 20))
        plant(b, g, at[b][1], o[1], three(rng, -8))
        for t in range(4):
            for r in range(N):
                v = runs(rng, t)
                for i, j in enumerate(np.sort(at[r][3 + 5 * t:8 + 5 * t])): plant(r, g, j, o[3 + t], v[i])
        first = int(firsts[g])
        v = np.zeros((8, 4))
        v[7] = 11 * 2.0 ** (4 + rng.permutation([-1, 0, 0, 1]))
        plant(first, g, at[first][23], o[7], v)
        for r in range(first + 1, N):
            v = np.zeros((8, 4))
            v[:7] = three(rng, 20, (7, 4))
            plant(r, g, at[r][23], o[7], v)
            keys[0, r, g, at[r][23]] = o[8]
    return planted(rng, x, keys[0], second=keys[1])
def setup_inputs_spread(rng):
    d = setup_inputs(rng)
    x = wide(rng, N, 128, 4 * C).astype(np.float32) * np.repeat(np.exp2(rng.integers(-4, 5, (N, 1, C))), 4, axis=-1).astype(np.float32)
    d["x"] = np.array(mx_ref.flush(x.astype(BF)))
    return d
def check_inputs(d):
    b = []
    for k in ("x", "u", "v"):
        a = np.abs(d[k].astype(np.float32))
        if not (np.isfinite(a).all() and ((a == 0) | (a >= 2.0 ** -30) & (a <= 2.0 ** 30)).all()): b.append("a value of " + k)
    for k in ("u", "v"):
        a = d[k].astype(np.float32)
        if not (a == a[:1]).all(): b.append(k + " differs between ranks")
    if (d["wc"] != d["wc"][:1]).any(): b.append("wc differs between ranks")
    s = [mx_ref.live(p) for p in d["ws"]]
    if any((p != s[0]).any() for p in s): b.append("ws differs between ranks")
    if ((d["wc"] & 127) == 127).any(): b.append("a code of wc")
    a = np.max(np.abs(decode(pk(d["wc"][0], d["ws"][0]))).reshape(16, 8, -1, 4), axis=(1, 3))
    if not ((a == 0) | (a >= 2.0 ** -30) & (a <= 2.0 ** 30)).all(): b.append("a block of W")
    return b
def reference(x, u, v, wc, ws):
    w, qu, qv = pk(wc[0], ws[0]), mx_ref.quantize(u[0]), mx_ref.quantize(v[0])
    now = [mx_ref.quantize(x[r]) for r in range(N)]
    for t in range(R):
        p, key, last = [], [], []
        for r in range(N):
            key.append(key_of(mx_ref.matmul(qu, now[r])))
            made = tile([mx_ref.matmul(pick(w, np.arange(128 * b, 128 * b + 128)), now[r]) * np.float32(0.03125) for b in range(4)])
            p.append(parts(made.astype(np.float32)))
            h = scan(p[r], key[r], np.zeros((8, K, 16, 4), np.float32))[1]
            last.append(mx_ref.quantize(whole(h).astype(BF)))
        came = decode(join(*last))
        c, before = np.zeros((128, 4 * K), np.float32), []
        for r in range(N):
            before.append(mx_ref.quantize(c.astype(BF)))
            c = np.maximum(np.float32(0.5) * c, cut(came, r, 4 * K))
        start = decode(join(*before))
        for r in range(N):
            h = scan(p[r], key[r], parts(np.ascontiguousarray(cut(start, r, 4 * K))))[0]
            now[r] = mx_ref.quantize(whole(h).astype(BF))
    y = np.zeros((N, 128, C), np.float32)
    oc, osc = np.zeros((N, 128, 4 * C), np.uint8), np.zeros((N, 16, C), np.uint8)
    for r in range(N):
        y[r] = mx_ref.matmul(qv, now[r])
        oc[r], osc[r] = emit(now[r])
    return {"y": y, "oc": oc, "osc": osc}

from concourse.bass import DstId, RemoteDMATransfer
from concourse.mybir import dt, AluOpType, ActivationFunctionType

ALU = AluOpType
ACT = ActivationFunctionType
C = 448
K = 64
SL = C + K
R = 2
HF = "float16"
MX = "float8_e4m3fn_x4"


def _sb(n, d):
    return ("sbuf", [128, n], d)


SCRATCH = {
    "xt": _sb(4 * C, "bfloat16"), "ut": _sb(512, "bfloat16"), "vt": _sb(512, "bfloat16"),
    "qu": _sb(128, MX), "su": _sb(128, "uint8"), "qv": _sb(128, MX), "sv": _sb(128, "uint8"),
    "qw": _sb(512, MX), "sw": _sb(512, "uint8"),
    "qa0": _sb(C, MX), "sa0": _sb(C, "uint8"), "qa1": _sb(C, MX), "sa1": _sb(C, "uint8"),
    "qa2": _sb(C, MX), "sa2": _sb(C, "uint8"),
    "ql0": _sb(9 * K, MX), "sl0": _sb(9 * K, "uint8"), "ql1": _sb(9 * K, MX), "sl1": _sb(9 * K, "uint8"),
    "qc0": _sb(128, MX), "sc0": _sb(128, "uint8"), "qc1": _sb(128, MX), "sc1": _sb(128, "uint8"),
    "qe": _sb(512, MX), "se": _sb(512, "uint8"), "eb": _sb(2048, "bfloat16"), "idn": _sb(128, "bfloat16"),
    "pi": _sb(1, "int32"), "qhi": _sb(2, "int32"), "qh": _sb(2, "float32"), "col": _sb(16, "float32"),
    "t16": _sb(16, "bfloat16"), "kcol": _sb(4, "bfloat16"), "sgb": _sb(4, "float32"), "nic": _sb(4, "float32"),
    "dga": _sb(16, "bfloat16"), "dgb": _sb(16, "bfloat16"), "dg": _sb(SL, "bfloat16"), "iot": _sb(C, "bfloat16"),
    "ks0": _sb(C, "bfloat16"), "kh": _sb(C, "bfloat16"), "neg1": _sb(C, "bfloat16"), "ttd": _sb(928, "bfloat16"),
    "bt": _sb(C, "bfloat16"), "btt": _sb(C, "bfloat16"), "ksum": _sb(C + 16, "bfloat16"), "kb0": _sb(C, "bfloat16"),
    "kb": _sb(C, "bfloat16"), "junk": _sb(C, "bfloat16"), "acc": _sb(4, "float32"), "ni": _sb(4, "float32"),
    "d5": _sb(5 * C, "bfloat16"), "nc5": _sb(5 * C, HF), "sel": _sb(5 * C + 160, HF), "tt": _sb(928, HF),
    "tto": _sb(928, HF), "ab": _sb(28, "float32"), "lst": _sb(32, "uint16"), "enl": _sb(4, "uint16"),
    "inv": _sb(SL, "bfloat16"), "invo": _sb(SL, HF), "ls": _sb(32, "uint16"), "dec": _sb(SL, "bfloat16"),
    "pp": _sb(4 * SL, "bfloat16"), "srt": _sb(4 * SL, "bfloat16"), "hs": _sb(4 * SL, "bfloat16"),
    "et": _sb(512, "bfloat16"), "ct": _sb(512, "bfloat16"), "cb": _sb(4 * K, "bfloat16"), "ht": _sb(4 * C, "bfloat16"),
    "yt": _sb(C, "float32"), "ps": ("psum", [128, 4096], "float32"),
}
_DMAS = ["dx0", "dx1", "du", "dv", "dwc", "dws", "doc0", "doc1", "dos0", "dos1", "dos2", "dos3", "dy0", "dy1"]
SEMAPHORES = (["cv", "ca", "cp", "cg", "sent"] + _DMAS + ["arr%d_%d" % (t, s) for t in range(R) for s in range(7)])


def _masks(topo, cores, src):
    c = cores[src]
    own = topo.cores_of(c)
    near = [d for d in range(src + 1, len(cores)) if cores[d] in own]
    far = [d for d in range(src + 1, len(cores)) if cores[d] not in own]
    out, used = [], []
    if far:
        used = topo.engines(c, cores[far[0]])
        out.append((far, used[0::2], used[1::2]))
    if near:
        e = [x for x in topo.engines(c, cores[near[0]]) if x not in used]
        out.append((near, e[0::2], e[1::2]))
    return out


def _bits(engines):
    m = 0
    for e in engines:
        m |= 1 << e
    return m


def rank_program(g, core, T, topo):
    rank = T.rank_of(core)
    if rank is None:
        return
    cores = list(T.cores)
    n_ranks = len(cores)
    last = rank == n_ranks - 1
    ops = []

    def v(name, lo=0, hi=None, step=1):
        if hi is None:
            hi = SCRATCH[name][1][1]
        ap = T[name][:, lo:hi:step] if step != 1 else T[name][:, lo:hi]
        if name == "ps":
            return (ap, name, frozenset(range(lo // 512, (hi - 1) // 512 + 1)))
        return (ap, name, frozenset(range(lo, hi, step)))

    def emit(q, call, reads, writes, sem=None, waits=()):
        ops.append([q, call, [(r[1], r[2]) for r in reads], [(w[1], w[2]) for w in writes], sem, list(waits)])

    def aps(*xs):
        return [x for x in xs if isinstance(x, tuple)]

    def a(x):
        return x[0] if isinstance(x, tuple) else x

    def memset(out, val):
        emit("v", lambda: g.vector.memset(out[0], val), [], [out])

    def ts(out, in0, s1, op0, s2=None, op1=None):
        if op1 is None:
            emit("v", lambda: g.vector.tensor_scalar(out[0], in0[0], a(s1), None, op0), aps(in0, s1), [out])
        else:
            emit("v", lambda: g.vector.tensor_scalar(out[0], in0[0], a(s1), a(s2), op0, op1), aps(in0, s1, s2), [out])

    def tt(out, in0, in1, op):
        emit("v", lambda: g.vector.tensor_tensor(out[0], in0[0], in1[0], op), [in0, in1], [out])

    def copy(out, in0):
        emit("v", lambda: g.vector.tensor_copy(out[0], in0[0]), [in0], [out])

    def scan(out, d0, d1, init, op0, op1):
        emit("v", lambda: g.vector.tensor_tensor_scan(out[0], d0[0], d1[0], a(init), op0, op1), aps(d0, d1, init), [out])

    def turn(out, in0):
        emit("v", lambda: g.vector.transpose(out[0], in0[0]), [in0], [out])

    def quant(q, s, in0):
        emit("v", lambda: g.vector.quantize_mx(q[0], s[0], in0[0]), [in0], [q, s])

    def act(out, in0, func, bias=0.0, scale=1.0, accum=None):
        if accum is None:
            emit("a", lambda: g.scalar.activation(out[0], in0[0], func, bias=a(bias), scale=scale), aps(in0, bias), [out])
        else:
            emit("a", lambda: g.scalar.activation(out[0], in0[0], func, bias=a(bias), scale=scale, accum_out=accum[0]),
                 aps(in0, bias), [out, accum])

    def fill(out, n, val):
        act(out, v("ks0", 0, n), ACT.Identity, bias=val, scale=0.0)

    def gather(q, out, win, off):
        if q == "v":
            emit("v", lambda: g.vector.tensor_copy(out[0], win[0].indirect(off[0])), [win, off], [out])
        else:
            emit("a", lambda: g.scalar.activation(out[0], win[0].indirect(off[0]), ACT.Copy), [win, off], [out])

    def scatter(win, off, in0):
        emit("v", lambda: g.vector.tensor_copy(win[0].indirect(off[0]), in0[0]), [in0, off], [win])

    def mm(bank, n, lq, ls, rq, rs, waits=()):
        out = v("ps", 512 * bank, 512 * bank + n)
        emit("p", lambda: g.tensor.matmul_mx(out[0], lq[0], ls[0], rq[0], rs[0], True, True), [lq, ls, rq, rs], [out], waits=waits)

    def dma(q, sem, out, in_, reads, writes):
        eng = g.sync if q == "s" else g.scalar
        emit(q, lambda: eng.dma_start(out, in_), reads, writes, sem=sem)

    def bank(b, n, lo=0):
        return v("ps", 512 * b + lo, 512 * b + lo + n)

    def lane(name, b, lo=0, hi=SL):
        return v(name, SL * b + lo, SL * b + hi)

    def col(i):
        return v("col", i, i + 1)

    hc = C // 2

    def half(name, i, w=1):
        return v(name, w * hc * i, w * hc * (i + 1))

    dma("a", "du", T.ut[:], T.u[:], [], [v("ut")])
    for i in range(2):
        dma("s", "dx%d" % i, half("xt", i, 4)[0], T.x[:, 4 * hc * i:4 * hc * (i + 1)], [], [half("xt", i, 4)])
    dma("s", "dwc", T.qw[:].bitcast(dt.uint8), T.wc[:], [], [v("qw")])
    dma("s", "dws", T.sw[:], T.ws[:], [], [v("sw")])
    dma("s", "dv", T.vt[:], T.v[:], [], [v("vt")])

    emit("g", lambda: g.iota(T.pi[:], [[0, 1]], 0, 1), [], [v("pi")])
    emit("g", lambda: g.iota(T.t16[:], [[1, 16]], 0, 0, allow_small_or_imprecise_dtypes=True), [], [v("t16")])
    emit("g", lambda: g.iota(T.iot[:], [[1, C]], -256, 0, allow_small_or_imprecise_dtypes=True), [], [v("iot")])
    memset(v("ks0"), 0.5)
    memset(v("kh"), 0.0)
    ts(v("qhi", 0, 1), v("pi"), 15, ALU.bitwise_and)
    ts(v("qhi", 1, 2), v("pi"), 4, ALU.logical_shift_right, 1, ALU.bitwise_and)
    memset(v("ks0", 0, C, 16), 0.0)
    copy(v("qh"), v("qhi"))
    memset(v("kh", 0, C, 16), -256.0)
    memset(v("kh", 1, C, 16), 64.0)
    qf, hf = v("qh", 0, 1), v("qh", 1, 2)
    ts(col(0), qf, 0.0, ALU.not_equal, 64.0, ALU.mult)
    ts(col(2), qf, -4.0, ALU.mult, -224.0, ALU.add)
    ts(col(3), qf, 15.0, ALU.is_lt, -1024.0, ALU.mult)
    ts(col(9), qf, 1.0, ALU.add)
    ts(col(1), qf, 4.0, ALU.mult, col(0), ALU.add)
    ts(v("dga"), v("t16"), qf, ALU.is_equal, -4096.0, ALU.mult)
    ts(v("dgb"), v("t16"), col(9), ALU.is_equal, 1024.0, ALU.mult)
    ts(v("nic"), v("t16", 0, 4), -1.0, ALU.mult, col(2), ALU.add)
    ts(v("kcol"), v("t16", 0, 4), col(1), ALU.add)
    ts(v("sgb"), v("t16", 0, 4), col(1), ALU.add, -0.5, ALU.add)
    tt(v("dg", 0, 16), v("dga"), v("dgb"), ALU.add)
    memset(v("ksum", C, C + 16), 0.0)
    memset(v("ksum", hc, hc + 16), 0.0)
    ts(v("nc5", 0, 5 * C, 5), v("ks0"), 0.0, ALU.mult, -2048.0, ALU.add)
    ts(v("sel", 0, 80), v("ks0", 0, 80), 0.0, ALU.mult)
    ts(v("sel", 80 + 5 * C, 160 + 5 * C), v("ks0", 0, 80), 0.0, ALU.mult)
    fill(v("neg1"), C, -1.0)
    fill(v("d5", 0, 5 * C, 5), C, 1.0)
    fill(v("ttd", 0, C), C, 0.0)
    fill(v("ttd", C, 2 * C), C, 0.0)
    fill(v("ttd", 2 * C, 928), 32, 0.0)
    for i, (s, b) in enumerate(((5120.0, -4096.0), (-4096.0, 0.0), (4096.0, -4096.0), (-5120.0, 1024.0))):
        act(col(4 + i), hf, ACT.Identity, bias=b, scale=s)
    act(col(8), col(3), ACT.Identity, bias=256.0)
    for b in range(4):
        fill(lane("pp", b, C, SL), K, 0.0)
    fill(v("ttd", 0, 480, 32), 15, col(4))
    fill(v("ttd", 16, 480, 32), 15, col(5))
    fill(v("ttd", 480, 928, 32), 14, col(6))
    fill(v("ttd", 496, 928, 32), 14, col(7))
    if rank > 0:
        emit("g", lambda: g.affine_select(T.idn[:], T.neg1[:, 0:128], [[-1, 128]], ALU.is_equal, 0.0, 0, 1),
             [v("neg1", 0, 128)], [v("idn")])

    def blank():
        fill(v("inv", 0, 256), 256, 192.0)
        fill(v("inv", 256, SL), 256, 192.0)

    def keys(i):
        lo = hc * i
        return [lambda: ts(half("bt", i), bank(5 + i, hc), 0.0, ALU.is_lt, 32.0, ALU.mult),
                lambda: turn(half("btt", i), half("bt", i)),
                lambda: scan(half("ksum", i), half("ks0", i), half("btt", i), 0.0, ALU.mult, ALU.add),
                lambda: scan(half("kb0", i), half("kh", i), v("ksum", lo + 5, lo + 5 + hc), 0.0, ALU.add, ALU.max),
                lambda: turn(half("kb", i), half("kb0", i))]

    def state(t, i, src):
        quant(half("qa%d" % t, i), half("sa%d" % t, i), half(src, i, 4))
        side = "u" if t < R else "v"
        mm(5 + i, hc, v("q" + side), v("s" + side), half("qa%d" % t, i), half("sa%d" % t, i))

    quant(v("qu"), v("su"), v("ut"))
    state(0, 0, "xt")
    for f in keys(0):
        f()
    state(0, 1, "xt")

    plan = [_masks(topo, cores, s) for s in range(n_ranks)]

    def arrival(src):
        for ds, ec, es in plan[src]:
            if rank in ds:
                return len(ec) + len(es)

    sent = [0]

    def send(t):
        lo = K * rank
        for which, name in ((1, "ql%d" % t), (2, "sl%d" % t)):
            src = v(name, lo, lo + K)
            view = src[0].bitcast(dt.uint8) if which == 1 else src[0]
            trs = []
            for p in plan[rank]:
                ids = [topo.addr(cores[d], core) for d in (p[0] if t == 0 else p[0][::-1])]
                trs.append(RemoteDMATransfer(dst_ids=[DstId(rid=i[0], pnc=i[1]) for i in ids], dma_engine_mask=_bits(p[which]),
                                             remote_sem=T.sem["arr%d_%d" % (t, rank)], srcs=[view], dsts=[view] * len(ids)))
                sent[0] += len(p[which])
            emit("r", lambda trs=trs: g.remote_dma_fused(trs, local_sem=T.sem.sent), [src], [])

    for t in range(R):
        qa, sa = v("qa%d" % t), v("sa%d" % t)
        ql, sl = "ql%d" % t, "sl%d" % t
        for b in range(4):
            mm(1 + b, C, v("qw", 128 * b, 128 * b + 128), v("sw", 128 * b, 128 * b + 128), qa, sa)
        if t == 0:
            for f in keys(1):
                f()
        else:
            k0, k1 = keys(0), keys(1)
            for f in (k0[0], k0[1], k1[0], k0[2], k1[1], k0[3], k1[2], k0[4], k1[3], k1[4]):
                f()
        early = 0 if t == 0 else 3
        for b in range(early):
            act(lane("pp", b, 0, C), bank(1 + b, C), ACT.Copy, scale=0.03125)
        for m in (0, 2):
            act(v("junk"), v("kb"), ACT.Sign, bias=v("sgb", m, m + 1), scale=-1.0, accum=v("acc", m, m + 1))
        for b in range(early, 4):
            act(lane("pp", b, 0, C), bank(1 + b, C), ACT.Copy, scale=0.03125)
        blank()
        if t == 0:
            n = 16
            while n < SL:
                act(v("dg", n, 2 * n), v("dg", 0, n), ACT.Copy)
                n *= 2
            fill(v("et", 0, 256), 256, 0.0)
            fill(v("et", 256, 512), 256, 0.0)
            if rank > 0:
                fill(v("ct", 256, 512), 256, 0.0)
                for i in range(0, 2048, C):
                    fill(v("eb", i, min(i + C, 2048)), min(C, 2048 - i), 0.0)
                for b in range(4):
                    act(v("eb", 513 * b, 512 * b + 512, 4), v("idn"), ACT.Copy, scale=-1.0)

        def five(name, m):
            return v(name, 4 - m, 5 * C, 5)

        def ni(m):
            return v("ni", 3 - m, 4 - m)

        def differs(m):
            ts(five("d5", m), v("kb"), v("kcol", m, m + 1), ALU.not_equal)

        def start(m):
            ts(ni(m), v("acc", m, m + 1), -0.5, ALU.mult, v("nic", m, m + 1), ALU.add)

        def follow(m):
            e = 5 * C - m
            ts(ni(m), v("nc5", e, e + 1), -1.0, ALU.add)

        def count(m):
            scan(five("nc5", m), five("d5", m), v("neg1"), ni(m), ALU.add, ALU.add)

        differs(0)
        differs(2)
        differs(1)
        start(0)
        differs(3)
        count(0)
        start(2)
        follow(1)
        count(2)
        count(1)
        follow(3)
        count(3)
        ts(v("lst", 28, 32), v("ni"), -1.0, ALU.mult)
        scan(v("sel", 80, 80 + 5 * C), v("d5"), v("nc5"), 0.0, ALU.mult, ALU.min)
        if not last:
            ts(v("enl"), v("nc5", 5 * C - 4, 5 * C), -1.0, ALU.mult)
        turn(v("tt", 0, 480), v("sel", 4, 5 * C + 160, 5))
        turn(v("tt", 480, 928), v("sel", 84, 5 * C + 80, 5))
        scan(v("tto", 0, 480), v("ttd", 0, 480), v("tt", 0, 480), 0.0, ALU.add, ALU.max)
        scan(v("tto", 480, 928), v("ttd", 480, 928), v("tt", 480, 928), 0.0, ALU.add, ALU.max)
        ra, rb = v("tto", 511, 928, 32), v("tto", 47, 480, 32)
        tt(v("ab", 0, 14), ra, rb, ALU.max)
        tt(v("ab", 14, 28), ra, rb, ALU.min)
        ts(v("lst", 0, 28, 2), v("ab", 0, 14), -1.0, ALU.mult, 1024.0, ALU.add)
        ts(v("lst", 1, 28, 2), v("ab", 14, 28), -1.0, ALU.mult)
        scatter(v("inv"), v("lst", 0, 28), v("iot"))
        scan(v("invo"), v("dg"), v("inv"), 0.0, ALU.add, ALU.max)
        cs = v("lst", 28, 32)
        ts(v("ls"), v("invo", 15, SL, 16), col(8), ALU.add)
        ts(v("dec"), v("inv"), 192.0, ALU.is_lt, 0.5, ALU.mult)

        def decay(b):
            scan(lane("hs", b), v("dec"), lane("srt", b), 0.0, ALU.mult, ALU.max)

        def end(q, b):
            gather(q, v("et", b, 256, 4), lane("hs", b), v("enl"))

        gather("a", lane("srt", 0), lane("pp", 0), v("ls"))
        gather("a", lane("srt", 1), lane("pp", 1), v("ls"))
        gather("v", lane("srt", 2), lane("pp", 2), v("ls"))
        if last:
            gather("v", lane("srt", 3), lane("pp", 3), v("ls"))
        else:
            decay(2)
            decay(0)
            gather("v", lane("srt", 3, 0, 256), lane("pp", 3), v("ls", 0, 16))
            gather("a", lane("srt", 3, 256, SL), lane("pp", 3), v("ls", 16, 32))
            decay(1)
            end("v", 2)
            decay(3)
            end("a", 0)
            end("a", 1)
            end("v", 3)
        quant(v(ql, K * rank, K * rank + 128), v(sl, K * rank, K * rank + 128), v("et"))
        if not last:
            send(t)
        if t == 0:
            if rank > 0:
                quant(v("qe"), v("se"), v("eb"))
            quant(v("qv"), v("sv"), v("vt"))

        if rank > 0:
            down = t == 0
            if down:
                sets = [(i, [i]) for i in range(rank - 1, -1, -1)]
            else:
                sets = [(0, list(range(min(2, rank))))] + [(i - 1, [i]) for i in range(2, rank)]
            nb, first = 0, True
            for s, members in sets:
                w = [("arr%d_%d" % (t, i), arrival(i)) for i in members]
                for b in range(4):
                    mm(nb + b, 128, v("qe", 128 * b, 128 * b + 128), v("se", 128 * b, 128 * b + 128),
                       v(ql, K * s, K * s + 128), v(sl, K * s, K * s + 128), waits=w if b == 0 else ())
                for i in members:
                    if not first:
                        ts(v("ct", 0, 256), v("ct", 0, 256), 2.0 if down else 0.5, ALU.mult)
                    for b in range(4):
                        d = bank(nb + b, K, K * (i - s))
                        if first:
                            copy(v("ct", b, 256, 4), d)
                        else:
                            tt(v("ct", b, 256, 4), d, v("ct", b, 256, 4), ALU.max)
                    first = False
                nb = 4 - nb
            if down and rank > 1:
                ts(v("ct", 0, 256), v("ct", 0, 256), 2.0 ** (1 - rank), ALU.mult)
            qc, sc = v("qc%d" % t), v("sc%d" % t)
            quant(qc, sc, v("ct"))
            for b in range(4):
                mm(nb + b, 128, v("qe", 128 * b, 128 * b + 128), v("se", 128 * b, 128 * b + 128), qc, sc)
            for b in range(4):
                act(v("cb", K * b, K * b + K), bank(nb + b, K), ACT.Copy)
            scatter(lane("srt", 0), cs, v("cb", 0, K))
            scatter(lane("srt", 1), cs, v("cb", K, 2 * K))
            decay(0)
            decay(1)
            scatter(lane("srt", 2), cs, v("cb", 2 * K, 3 * K))
            scatter(lane("srt", 3), cs, v("cb", 3 * K, 4 * K))
            decay(2)
            decay(3)

        def back(q, b, i):
            gather(q, v("ht", 4 * hc * i + b, 4 * hc * (i + 1), 4), lane("hs", b), v("lst", 14 * i, 14 * i + 14))

        if rank > 0:
            steps = ("a00", "a10", "a01", "a20", "v30", "q", "a11", "a21", "v31")
        else:
            steps = ("a00", "a10", "v20", "v30", "q", "a01", "a11", "v21", "v31")
        for st in steps:
            if st == "q":
                state(t + 1, 0, "ht")
            else:
                back(st[0], int(st[1]), int(st[2]))
        state(t + 1, 1, "ht")

    for i in range(2):
        dma("s", "doc%d" % i, T.oc[:, 4 * hc * i:4 * hc * (i + 1)], half("qa2", i)[0].bitcast(dt.uint8), [half("qa2", i)], [])
        act(half("yt", i), bank(5 + i, hc), ACT.Copy)
        dma("a", "dy%d" % i, T.y[:, hc * i:hc * (i + 1)], half("yt", i)[0], [half("yt", i)], [])
    for k in range(4):
        dma("s", "dos%d" % k, T.osc[4 * k:4 * k + 4, :], T.sa2[32 * k:32 * k + 4, :], [v("sa2")], [])

    def queue(o):
        return "g" if o[0] == "r" else o[0]

    def meets(xs, ys):
        return any(n1 == n2 and not p1.isdisjoint(p2) for n1, p1 in xs for n2, p2 in ys)

    deps = []
    for i, o in enumerate(ops):
        best, extra = {}, []
        for j in range(i):
            p = ops[j]
            if p[0] == "r":
                continue
            hit = meets(p[3], o[2]) or meets(p[3], o[3]) or meets(p[2], o[3])
            if not hit and p[0] != o[0]:
                hit = meets([x for x in p[2] if x[0] == "ps"], o[2])
            if hit:
                if p[4] is None:
                    best[p[0]] = j
                else:
                    extra.append(j)
        deps.append((best, extra))
    known, need, seen = {}, [], []
    for i, o in enumerate(ops):
        k = known.setdefault(queue(o), {})
        w = []
        best, extra = deps[i]
        for j in sorted(list(best.values()) + extra, reverse=True):
            key = ops[j][4] or ops[j][0]
            if k.get(key, -1) < j:
                w.append(j)
                k[key] = j
                for kk, vv in seen[j].items():
                    if k.get(kk, -1) < vv:
                        k[kk] = vv
        need.append(w)
        seen.append(dict(k))
    wanted = set(j for w in need for j in w)
    counts, value = {}, {}
    engines = {"v": g.vector, "a": g.scalar, "p": g.tensor, "s": g.sync, "g": g}
    for i, o in enumerate(ops):
        e = engines[queue(o)]
        for name, n in o[5]:
            e.wait_ge(T.sem[name], n)
        for j in need[i]:
            e.wait_ge(T.sem[value[j][0]], value[j][1])
        ins = o[1]()
        if o[4] is not None:
            ins.then_inc(T.sem[o[4]], 16)
            value[i] = (o[4], 16)
        elif i in wanted:
            counts[o[0]] = counts.get(o[0], 0) + 1
            ins.then_inc(T.sem["c" + o[0]], 1)
            value[i] = ("c" + o[0], counts[o[0]])
    for i, o in enumerate(ops):
        if o[4] is not None and i not in wanted:
            g.sync.wait_ge(T.sem[o[4]], 16)
    if sent[0]:
        g.wait_ge(T.sem.sent, sent[0])
